import numpy as np
import ml_dtypes


def mxq(x, axis, fmt="e4m3"):
    dtype, down = {"e4m3": (ml_dtypes.float8_e4m3fn, 7), "e5m2": (ml_dtypes.float8_e5m2, 14)}[fmt]
    v = np.moveaxis(np.asarray(x, np.float32).astype(ml_dtypes.bfloat16).astype(np.float64), axis, -1)
    blocks = v.reshape(v.shape[:-1] + (-1, 32))
    amax = np.abs(blocks).max(-1, keepdims=True)
    byte = np.maximum(np.where(amax > 0, np.frexp(amax)[1] - 1 + 127, 0) - down, 1)
    scale = np.exp2(byte - 127.0)
    codes = (blocks / scale).astype(np.float32).astype(dtype).astype(np.float64)
    return np.moveaxis((codes * scale).reshape(v.shape), -1, axis)


WIDE = False


def mx_kscale(k):
    if not WIDE:
        return np.ones(k)
    levels = np.array([10, -10, 5, -5, 0])
    if k % 512:
        return np.exp2(np.random.permutation(np.resize(levels, k // 32))).repeat(32)
    a = np.empty((k // 512, 16))
    for p in range(k // 512):
        a[p, :8] = np.random.permutation(np.resize(levels, 8))
        for g in range(8):
            far = levels[np.abs(levels - a[p, g]) >= 10]
            a[p, g + 8] = far[np.random.randint(len(far))]
    return np.exp2(a.ravel()).repeat(32)


def f64(x):
    return np.asarray(x).astype(np.float64)


def striped8(idx):
    return np.asarray(idx).reshape(8, -1, 16).transpose(0, 2, 1).reshape(128, -1).astype(np.uint16)


def unstriped8(offs):
    return offs.reshape(8, 16, -1).transpose(0, 2, 1).reshape(8, -1).astype(np.int64)


def pick8(x, idx, run):
    r = np.arange(len(x))
    return x[r[:, None], idx[r % (8 * run) // run]]


E2M1 = np.array([0.0, 0.5, 1.0, 1.5, 2.0, 3.0, 4.0, 6.0, -0.0, -0.5, -1.0, -1.5, -2.0, -3.0, -4.0, -6.0])


def pack_weight(w, fmt):
    k, n = w.shape
    w = f64(np.asarray(w, np.float32).astype(ml_dtypes.bfloat16)).reshape(k // 32, 32, n)
    amax = np.abs(w).max(1)
    if fmt == "e4m3":
        byte = np.frexp(amax)[1] - 1 + 127 - 7
    else:
        mant, ex = np.frexp(amax / 6.0)
        byte = np.where(mant > 0.5, ex, ex - 1) + 127
    byte = np.clip(np.where(amax > 0, byte, 1), 1, 254)
    scaled = (w * np.exp2(127.0 - byte)[:, None, :]).reshape(k, n).astype(np.float32)
    by_word = np.ascontiguousarray(scaled.reshape(k // 512, 128, 4, n).transpose(0, 1, 3, 2))
    if fmt == "e4m3":
        words = by_word.astype(ml_dtypes.float8_e4m3fn).view(np.uint8)
    else:
        c = by_word.astype(ml_dtypes.float4_e2m1fn).view(np.uint8) & 0xF
        words = (c[..., 0::2] | (c[..., 1::2] << 4)).reshape(k // 512, 128, 2 * n)
    return np.ascontiguousarray(words), np.ascontiguousarray(byte.astype(np.uint8).reshape(k // 512, 16, n))


def unpack_weight(words, scales, fmt):
    g, _, n = scales.shape
    words = np.ascontiguousarray(words).reshape(g, 128, n, -1)
    if fmt == "e4m3":
        vals = words.view(ml_dtypes.float8_e4m3fn).astype(np.float64)
    else:
        nib = np.empty((g, 128, n, 4), np.uint8)
        nib[..., 0::2] = words & 0xF
        nib[..., 1::2] = words >> 4
        vals = E2M1[nib]
    vals = vals * np.repeat(np.exp2(scales.astype(np.float64) - 127.0), 8, axis=1)[..., None]
    return vals.transpose(0, 1, 3, 2).reshape(g * 512, n)


D, V, Q, I, G = 512, 2048, 128, 512, 64


def setup_inputs():
    n = np.random.standard_normal
    idx = np.stack([np.random.permutation(V)[:I] for _ in range(8)])
    fd = mx_kscale(D)
    vocp = pack_weight(n((D, V)) / fd[:, None], "e2m1")
    return {
        "hid": (n((D, Q)) * 1.0 / np.sqrt(D) * fd[:, None]).astype(np.float32),
        "voc_words": vocp[0],
        "voc_scales": vocp[1],
        "aim": (np.random.uniform(0.3, 1.7, (Q, G))).astype(np.float32),
        "old": (0.5 * n((Q, V))).astype(np.float32),
        "offs": striped8(idx),
    }


def reference(hid, voc_words, voc_scales, aim, old, offs):
    idx = unstriped8(offs)
    vocu = unpack_weight(voc_words, voc_scales, "e2m1")
    hidq = mxq(f64(hid), 0, "e4m3")
    a = hidq.T @ vocu
    m1 = np.max(a, axis=1, keepdims=True)
    p = np.exp(a - m1)
    z = np.sum(p, axis=1, keepdims=True)
    px = np.exp(pick8(a, idx, 16) - m1)
    s1g = px.reshape(Q, G, I // G).sum(axis=2)
    u1 = s1g / z * 256.0 - f64(aim)
    du1 = u1 * 2.0
    ds1g = du1 * 256.0 / z
    r1 = np.repeat(ds1g, I // G, axis=1)
    dz = np.sum(du1 * 256.0 * s1g / np.square(z) * (-1.0), axis=1, keepdims=True)
    e2 = r1 * px
    s2 = np.zeros((Q, V))
    s2[np.arange(Q)[:, None], idx[np.arange(Q) % 128 // 16]] = e2
    da = dz * p + s2
    y = da + f64(old)
    return y

@@ -1,0 +1,179 @@
+from contextlib import ExitStack
+
+import concourse.mybir as mybir
+from concourse.masks import make_identity
+
+D, V, Q, I, G = 512, 2048, 128, 512, 64
+FLOPS = 2 * D * V * Q
+
+F32 = mybir.dt.float32
+BF16 = mybir.dt.bfloat16
+I32 = mybir.dt.int32
+U32 = mybir.dt.uint32
+U16 = mybir.dt.uint16
+U8 = mybir.dt.uint8
+FP8X4 = mybir.dt.float8_e4m3fn_x4
+FP4X4 = mybir.dt.float4_e2m1fn_x4
+ALU = mybir.AluOpType
+ACT = mybir.ActivationFunctionType
+AX = mybir.AxisListType
+
+P = 128
+BANK = 512
+NB = V // BANK
+PE_CHUNKS = [0, 1]
+G_CHUNKS = [3]
+OUT_ORDER = [(0, 0, 512), (1, 0, 512), (2, 0, 512), (3, 0, 256), (3, 256, 512)]
+WORD_LOADS = [(0, 512), (512, 1024), (1024, 2048)]
+SHADOW = [2]
+HALVES = 2
+
+
+def tile_attend_bgroupaims_heads_kernel(tc, hid, voc_words, voc_scales, aim, old, offs, out):
+    nc = tc.nc
+    with ExitStack() as ctx:
+        lists = ctx.enter_context(tc.tile_pool(name="lists", bufs=1))
+        sb = ctx.enter_context(tc.tile_pool(name="sb", bufs=1))
+        ps = ctx.enter_context(tc.psum_pool(name="ps", bufs=1))
+
+        hid_raw = sb.tile([P, 4, Q], F32)
+        nc.sync.dma_start(hid_raw[:], hid.rearrange("(p t) q -> p t q", t=4))
+        voc_plane = sb.tile([P, V], U8, align_bytes=64)
+        for quad in range(4):
+            nc.sync.dma_start(voc_plane[32 * quad : 32 * quad + 4, :].bitcast(I32),
+                              voc_scales[0, 4 * quad : 4 * quad + 4, :].bitcast(I32))
+        words = {}
+        for lo, hi in WORD_LOADS:
+            w = sb.tile([P, 2 * (hi - lo)], U8, align_bytes=64, name=f"words{lo}")
+            nc.sync.dma_start(w[:].bitcast(I32), voc_words[0, :, 2 * lo : 2 * hi].bitcast(I32))
+            for b in range(lo // BANK, hi // BANK):
+                words[b] = w[:, 2 * (b * BANK - lo) : 2 * ((b + 1) * BANK - lo)]
+        offsets = lists.tile([P, I // 16], U16)
+        nc.sync.dma_start(offsets[:], offs)
+        old_sb = [sb.tile([P, 2 * BANK], F32, name=f"old{h}") for h in range(2)]
+        for h in range(2):
+            nc.sync.dma_start(old_sb[h][:], old[:, 2 * h * BANK : 2 * (h + 1) * BANK])
+        aim_sb = sb.tile([P, G], F32)
+        nc.sync.dma_start(aim_sb[:], aim)
+
+        def old_cols(b, lo, hi):
+            return old_sb[b // 2][:, (b % 2) * BANK + lo : (b % 2) * BANK + hi]
+
+        s2 = sb.tile([P, V], F32)
+        nc.vector.memset(s2[:], 0.0)
+        ident = sb.tile([P, P], F32)
+        make_identity(nc, ident[:])
+
+
+        hid_bf = sb.tile([P, Q, 4], BF16, align_bytes=64)
+        nc.vector.tensor_copy(hid_bf[:].rearrange("p (c i) t -> p c t i", i=4),
+                              hid_raw[:].rearrange("p t (c i) -> p c t i", i=4))
+        hid_codes = sb.tile([P, Q], U32, align_bytes=64)
+        hid_plane = sb.tile([P, Q], U8, align_bytes=64)
+        nc.vector.quantize_mx(out=hid_codes[:].bitcast(FP8X4), scales=hid_plane[:],
+                              in_=hid_bf[:].rearrange("p q t -> p (q t)"))
+
+        a = sb.tile([P, V], F32)
+        p = sb.tile([P, V], F32)
+        m = sb.tile([P, NB], F32)
+        neg_m = sb.tile([P, NB], F32)
+        zb = sb.tile([P, NB], F32)
+        neg_m1 = sb.tile([P, 1], F32)
+        f = sb.tile([P, NB], F32)
+        nc.vector.memset(f[:, NB - 1 :], 1.0)
+        for b in range(NB):
+            cols = slice(b * BANK, (b + 1) * BANK)
+            bank = ps.tile([P, BANK], F32, name=f"score{b}")
+            nc.tensor.matmul_mx(out=bank[:], lhsT=hid_codes[:].bitcast(FP8X4), lhsT_scale=hid_plane[:],
+                                rhs=words[b].bitcast(FP4X4), rhs_scale=voc_plane[:, cols], start=True, stop=True)
+            nc.vector.tensor_scalar(a[:, cols], bank[:], 1.0, None, ALU.mult, ALU.max, accum_out=m[:, b : b + 1])
+            if b < NB - 1:
+                nc.gpsimd.tensor_scalar(neg_m[:, b : b + 1], m[:, b : b + 1], -1.0, 0.0, ALU.mult, ALU.add)
+                shift = neg_m[:, b : b + 1]
+            else:
+                nc.vector.tensor_reduce(neg_m1[:], m[:], AX.X, ALU.max, negate=True)
+                shift = neg_m1[:]
+            nc.scalar.activation(p[:, cols], a[:, cols], ACT.Exp, bias=shift, accum_out=zb[:, b : b + 1])
+
+        turned = {}
+        for b in PE_CHUNKS:
+            turned[b] = ps.tile([P, BANK], F32, name=f"turned{b}")
+            for j in range(4):
+                nc.tensor.matmul(turned[b][:, j * P : (j + 1) * P], old_cols(b, j * P, (j + 1) * P), ident[:],
+                                 start=(j == 0), stop=False, is_transpose=True)
+
+        nc.scalar.activation(f[:, : NB - 1], m[:, : NB - 1], ACT.Exp, bias=neg_m1[:])
+        n = I // HALVES
+        ag = sb.tile([P, I], F32)
+        px = sb.tile([P, I], F32)
+        for h in range(HALVES):
+            nc.vector.tensor_copy(ag[:, h * n : (h + 1) * n].bitcast(U32),
+                                  a[:].bitcast(U32).indirect(offsets[:, h * n // 16 : (h + 1) * n // 16]))
+            nc.scalar.activation(px[:, h * n : (h + 1) * n], ag[:, h * n : (h + 1) * n], ACT.Exp, bias=neg_m1[:])
+
+        zf = sb.tile([P, NB], F32)
+        z256 = sb.tile([P, 1], F32)
+        nc.vector.scalar_tensor_tensor(zf[:], zb[:], 1.0 / 256.0, f[:], ALU.mult, ALU.mult, accum_out=z256[:])
+        px3 = px[:].rearrange("p (g j) -> p g j", j=8)
+        s1g = sb.tile([P, G], F32)
+        gh = G // HALVES
+        nc.vector.tensor_reduce(s1g[:, :gh], px3[:, :gh, :], AX.X, ALU.add)
+        rz = sb.tile([P, 1], F32)
+        nc.vector.reciprocal(rz[:], z256[:])
+        for h in range(1, HALVES):
+            nc.vector.tensor_reduce(s1g[:, h * gh : (h + 1) * gh], px3[:, h * gh : (h + 1) * gh, :], AX.X, ALU.add)
+        c = sb.tile([P, 1], F32)
+        nc.scalar.mul(c[:], rz[:], 2.0)
+        nf = sb.tile([P, NB], F32)
+        nc.gpsimd.tensor_scalar(nf[:], f[:], rz[:], -1.0 / 256.0, ALU.mult, ALU.mult)
+
+        u1 = sb.tile([P, G], F32)
+        nc.vector.scalar_tensor_tensor(u1[:], s1g[:], rz[:], aim_sb[:], ALU.mult, ALU.subtract)
+        e2 = sb.tile([P, I], F32)
+        e_sum = sb.tile([P, 1], F32)
+        nc.vector.scalar_tensor_tensor(e2[:].rearrange("p (g j) -> p g j", j=8),
+                                       u1[:].unsqueeze(2).to_broadcast([P, G, 8]), c[:], px3,
+                                       ALU.mult, ALU.mult, accum_out=e_sum[:])
+        nc.vector.tensor_copy(s2[:].indirect(offsets[:]), e2[:])
+
+        dzb = sb.tile([P, NB], F32)
+        nc.scalar.activation(dzb[:], nf[:], ACT.Identity, scale=e_sum[:])
+        base = {}
+
+        def turn_in(b):
+            pd = sb.tile([P, BANK], F32, name=f"pd{b}")
+            nc.scalar.activation(pd[:], p[:, b * BANK : (b + 1) * BANK], ACT.Identity, scale=dzb[:, b : b + 1])
+            for j in range(4):
+                nc.tensor.matmul(turned[b][:, j * P : (j + 1) * P], pd[:, j * P : (j + 1) * P], ident[:],
+                                 start=False, stop=(j == 3), is_transpose=True)
+
+        def turn_back(b):
+            tsb = sb.tile([P, BANK], F32, name=f"tsb{b}")
+            nc.scalar.copy(tsb[:], turned[b][:])
+            base[b] = ps.tile([P, BANK], F32, name=f"score{b}")
+            for j in range(4):
+                nc.tensor.transpose(base[b][:, j * P : (j + 1) * P], tsb[:, j * P : (j + 1) * P], ident[:])
+
+        for b in PE_CHUNKS[:2]:
+            turn_in(b)
+        for b in SHADOW:
+            pd = sb.tile([P, BANK], F32, name=f"pd{b}")
+            nc.scalar.activation(pd[:], p[:, b * BANK : (b + 1) * BANK], ACT.Identity, scale=dzb[:, b : b + 1])
+            base[b] = sb.tile([P, BANK], F32, name=f"base{b}")
+            nc.gpsimd.tensor_tensor(base[b][:], pd[:], old_cols(b, 0, BANK), ALU.add)
+        turn_back(PE_CHUNKS[0])
+        for b in PE_CHUNKS[2:]:
+            turn_in(b)
+        for b in PE_CHUNKS[1:]:
+            turn_back(b)
+        for b in G_CHUNKS:
+            base[b] = sb.tile([P, BANK], F32, name=f"base{b}")
+            nc.gpsimd.tensor_tensor(base[b][:], s2[:, b * BANK : (b + 1) * BANK], old_cols(b, 0, BANK), ALU.add)
+        for b, lo, hi in OUT_ORDER:
+            cols = slice(b * BANK + lo, b * BANK + hi)
+            y = sb.tile([P, hi - lo], F32, name=f"y{b}_{lo}")
+            if b in G_CHUNKS:
+                nc.vector.scalar_tensor_tensor(y[:], p[:, cols], dzb[:, b : b + 1], base[b][:, lo:hi], ALU.mult, ALU.add)
+            else:
+                nc.vector.tensor_tensor(y[:], base[b][:, lo:hi], s2[:, cols], ALU.add)
+            nc.sync.dma_start(out[:, cols], y[:])

@@ -125,7 +125,9 @@ def tile_attend_bgroupaims_heads_kernel(tc, hid, voc_words, voc_scales, aim, old
         c = sb.tile([P, 1], F32)
         nc.scalar.mul(c[:], rz[:], 2.0)
         nf = sb.tile([P, NB], F32)
-        nc.gpsimd.tensor_scalar(nf[:], f[:], rz[:], -1.0 / 256.0, ALU.mult, ALU.mult)
+        neg_rz = sb.tile([P, 1], F32)
+        nc.scalar.mul(neg_rz[:], rz[:], -1.0 / 256.0)
+        nc.scalar.activation(nf[:], f[:], ACT.Identity, scale=neg_rz[:])
 
         u1 = sb.tile([P, G], F32)
         nc.vector.scalar_tensor_tensor(u1[:], s1g[:], rz[:], aim_sb[:], ALU.mult, ALU.subtract)
@@ -167,11 +169,15 @@ def tile_attend_bgroupaims_heads_kernel(tc, hid, voc_words, voc_scales, aim, old
         for b in PE_CHUNKS[1:]:
             turn_back(b)
         for b in G_CHUNKS:
-            base[b] = sb.tile([P, BANK], F32, name=f"base{b}")
+            base[b] = sb.tile([P, BANK], F32, name=f"pd{SHADOW[-1]}")
             nc.gpsimd.tensor_tensor(base[b][:], s2[:, b * BANK : (b + 1) * BANK], old_cols(b, 0, BANK), ALU.add)
+        y_tail = sb.tile([P, 2 * BANK], F32, name=f"tsb{PE_CHUNKS[-1]}")
         for b, lo, hi in OUT_ORDER:
             cols = slice(b * BANK + lo, b * BANK + hi)
-            y = sb.tile([P, hi - lo], F32, name=f"y{b}_{lo}")
+            if b in PE_CHUNKS:
+                y = sb.tile([P, hi - lo], F32, name=f"y{b}_{lo}")
+            else:
+                y = y_tail[:, (b - 2) * BANK + lo : (b - 2) * BANK + hi]
             if b in G_CHUNKS:
                 nc.vector.scalar_tensor_tensor(y[:], p[:, cols], dzb[:, b : b + 1], base[b][:, lo:hi], ALU.mult, ALU.add)
             else:

@@ -19,14 +19,24 @@ ACT = mybir.ActivationFunctionType
 AX = mybir.AxisListType
 
 P = 128
+PACK = 4
+FP4_WORD_BYTES = 2
+LIST_ROWS = 16
+GROUP = I // G
+SHARE_SCALE = 256.0
 BANK = 512
-NB = V // BANK
-PE_CHUNKS = [0, 1]
-G_CHUNKS = [3]
-OUT_ORDER = [(0, 0, 512), (1, 0, 512), (2, 0, 512), (3, 0, 256), (3, 256, 512)]
-WORD_LOADS = [(0, 512), (512, 1024), (1024, 2048)]
-SHADOW = [2]
-HALVES = 2
+BANKS = V // BANK
+LAST = BANKS - 1
+PIECE = BANK // 2
+WORD_LOADS = ((0, 512), (512, 1024), (1024, 2048))
+TENSOR_BANKS = (0, 1)
+GPSIMD_BANKS = (2, 3)
+HALF_SLOTS = I // 2
+HALF_GROUPS = G // 2
+
+
+def bank_cols(b, lo=0, hi=BANK):
+    return slice(b * BANK + lo, b * BANK + hi)
 
 
 def tile_attend_bgroupaims_heads_kernel(tc, hid, voc_words, voc_scales, aim, old, offs, out):
@@ -36,36 +46,35 @@ def tile_attend_bgroupaims_heads_kernel(tc, hid, voc_words, voc_scales, aim, old
         sb = ctx.enter_context(tc.tile_pool(name="sb", bufs=1))
         ps = ctx.enter_context(tc.psum_pool(name="ps", bufs=1))
 
-        hid_raw = sb.tile([P, 4, Q], F32)
-        nc.sync.dma_start(hid_raw[:], hid.rearrange("(p t) q -> p t q", t=4))
+        hid_raw = sb.tile([P, PACK, Q], F32)
+        nc.sync.dma_start(hid_raw[:], hid.rearrange("(p t) q -> p t q", t=PACK))
         voc_plane = sb.tile([P, V], U8, align_bytes=64)
-        for quad in range(4):
-            nc.sync.dma_start(voc_plane[32 * quad : 32 * quad + 4, :].bitcast(I32),
-                              voc_scales[0, 4 * quad : 4 * quad + 4, :].bitcast(I32))
+        for r in range(4):
+            nc.sync.dma_start(voc_plane[r:P:32, :].bitcast(I32), voc_scales[0, r:16:4, :].bitcast(I32))
         words = {}
         for lo, hi in WORD_LOADS:
-            w = sb.tile([P, 2 * (hi - lo)], U8, align_bytes=64, name=f"words{lo}")
-            nc.sync.dma_start(w[:].bitcast(I32), voc_words[0, :, 2 * lo : 2 * hi].bitcast(I32))
+            loaded = sb.tile([P, FP4_WORD_BYTES * (hi - lo)], U8, align_bytes=64, name=f"words{lo}")
+            nc.sync.dma_start(loaded[:].bitcast(I32),
+                              voc_words[0, :, FP4_WORD_BYTES * lo : FP4_WORD_BYTES * hi].bitcast(I32))
             for b in range(lo // BANK, hi // BANK):
-                words[b] = w[:, 2 * (b * BANK - lo) : 2 * ((b + 1) * BANK - lo)]
-        offsets = lists.tile([P, I // 16], U16)
+                words[b] = loaded[:, FP4_WORD_BYTES * (b * BANK - lo) : FP4_WORD_BYTES * ((b + 1) * BANK - lo)]
+        offsets = lists.tile([P, I // LIST_ROWS], U16)
         nc.sync.dma_start(offsets[:], offs)
-        old_sb = [sb.tile([P, 2 * BANK], F32, name=f"old{h}") for h in range(2)]
-        for h in range(2):
-            nc.sync.dma_start(old_sb[h][:], old[:, 2 * h * BANK : 2 * (h + 1) * BANK])
+        old_pairs = [sb.tile([P, 2 * BANK], F32, name=f"old{pair}") for pair in range(BANKS // 2)]
+        for pair in range(BANKS // 2):
+            nc.sync.dma_start(old_pairs[pair][:], old[:, 2 * pair * BANK : 2 * (pair + 1) * BANK])
         aim_sb = sb.tile([P, G], F32)
         nc.sync.dma_start(aim_sb[:], aim)
 
-        def old_cols(b, lo, hi):
-            return old_sb[b // 2][:, (b % 2) * BANK + lo : (b % 2) * BANK + hi]
+        def old_cols(b, lo=0, hi=BANK):
+            return old_pairs[b // 2][:, bank_cols(b % 2, lo, hi)]
 
         s2 = sb.tile([P, V], F32)
         nc.vector.memset(s2[:], 0.0)
         ident = sb.tile([P, P], F32)
         make_identity(nc, ident[:])
 
-
-        hid_bf = sb.tile([P, Q, 4], BF16, align_bytes=64)
+        hid_bf = sb.tile([P, Q, PACK], BF16, align_bytes=64)
         nc.vector.tensor_copy(hid_bf[:].rearrange("p (c i) t -> p c t i", i=4),
                               hid_raw[:].rearrange("p t (c i) -> p c t i", i=4))
         hid_codes = sb.tile([P, Q], U32, align_bytes=64)
@@ -75,111 +84,131 @@ def tile_attend_bgroupaims_heads_kernel(tc, hid, voc_words, voc_scales, aim, old
 
         a = sb.tile([P, V], F32)
         p = sb.tile([P, V], F32)
-        m = sb.tile([P, NB], F32)
-        neg_m = sb.tile([P, NB], F32)
-        zb = sb.tile([P, NB], F32)
+        m = sb.tile([P, BANKS], F32)
+        neg_m = sb.tile([P, BANKS], F32)
+        z_bank = sb.tile([P, BANKS], F32)
         neg_m1 = sb.tile([P, 1], F32)
-        f = sb.tile([P, NB], F32)
-        nc.vector.memset(f[:, NB - 1 :], 1.0)
-        for b in range(NB):
-            cols = slice(b * BANK, (b + 1) * BANK)
-            bank = ps.tile([P, BANK], F32, name=f"score{b}")
-            nc.tensor.matmul_mx(out=bank[:], lhsT=hid_codes[:].bitcast(FP8X4), lhsT_scale=hid_plane[:],
+        f = sb.tile([P, BANKS], F32)
+        nc.vector.memset(f[:, LAST:], 1.0)
+        for b in range(BANKS):
+            cols = bank_cols(b)
+            scores = ps.tile([P, BANK], F32, name=f"bank{b}")
+            nc.tensor.matmul_mx(out=scores[:], lhsT=hid_codes[:].bitcast(FP8X4), lhsT_scale=hid_plane[:],
                                 rhs=words[b].bitcast(FP4X4), rhs_scale=voc_plane[:, cols], start=True, stop=True)
-            nc.vector.tensor_scalar(a[:, cols], bank[:], 1.0, None, ALU.mult, ALU.max, accum_out=m[:, b : b + 1])
-            if b < NB - 1:
+            nc.vector.tensor_scalar(a[:, cols], scores[:], 1.0, None, ALU.mult, ALU.max, accum_out=m[:, b : b + 1])
+            if b < LAST:
                 nc.gpsimd.tensor_scalar(neg_m[:, b : b + 1], m[:, b : b + 1], -1.0, 0.0, ALU.mult, ALU.add)
                 shift = neg_m[:, b : b + 1]
             else:
                 nc.vector.tensor_reduce(neg_m1[:], m[:], AX.X, ALU.max, negate=True)
                 shift = neg_m1[:]
-            nc.scalar.activation(p[:, cols], a[:, cols], ACT.Exp, bias=shift, accum_out=zb[:, b : b + 1])
+                nc.scalar.activation(f[:, :LAST], m[:, :LAST], ACT.Exp, bias=neg_m1[:])
+            nc.scalar.activation(p[:, cols], a[:, cols], ACT.Exp, bias=shift, accum_out=z_bank[:, b : b + 1])
 
         turned = {}
-        for b in PE_CHUNKS:
-            turned[b] = ps.tile([P, BANK], F32, name=f"turned{b}")
-            for j in range(4):
-                nc.tensor.matmul(turned[b][:, j * P : (j + 1) * P], old_cols(b, j * P, (j + 1) * P), ident[:],
-                                 start=(j == 0), stop=False, is_transpose=True)
+        for b in TENSOR_BANKS:
+            for h in range(2):
+                turned[b, h] = ps.tile([P, PIECE], F32, name=f"turned{b}_{h}")
+                for j in range(2):
+                    nc.tensor.matmul(turned[b, h][:, j * P : (j + 1) * P],
+                                     old_cols(b, h * PIECE + j * P, h * PIECE + (j + 1) * P), ident[:],
+                                     start=(j == 0), stop=False, is_transpose=True)
 
-        nc.scalar.activation(f[:, : NB - 1], m[:, : NB - 1], ACT.Exp, bias=neg_m1[:])
-        n = I // HALVES
-        ag = sb.tile([P, I], F32)
+        a_listed = sb.tile([P, I], F32)
         px = sb.tile([P, I], F32)
-        for h in range(HALVES):
-            nc.vector.tensor_copy(ag[:, h * n : (h + 1) * n].bitcast(U32),
-                                  a[:].bitcast(U32).indirect(offsets[:, h * n // 16 : (h + 1) * n // 16]))
-            nc.scalar.activation(px[:, h * n : (h + 1) * n], ag[:, h * n : (h + 1) * n], ACT.Exp, bias=neg_m1[:])
+        for h in range(2):
+            slots = slice(h * HALF_SLOTS, (h + 1) * HALF_SLOTS)
+            half_list = offsets[:, h * HALF_SLOTS // LIST_ROWS : (h + 1) * HALF_SLOTS // LIST_ROWS]
+            nc.vector.tensor_copy(a_listed[:, slots].bitcast(U32), a[:].bitcast(U32).indirect(half_list))
+            nc.scalar.activation(px[:, slots], a_listed[:, slots], ACT.Exp, bias=neg_m1[:])
 
-        zf = sb.tile([P, NB], F32)
-        z256 = sb.tile([P, 1], F32)
-        nc.vector.scalar_tensor_tensor(zf[:], zb[:], 1.0 / 256.0, f[:], ALU.mult, ALU.mult, accum_out=z256[:])
-        px3 = px[:].rearrange("p (g j) -> p g j", j=8)
+        z_terms = sb.tile([P, BANKS], F32)
+        z_scaled = sb.tile([P, 1], F32)
+        nc.vector.scalar_tensor_tensor(z_terms[:], z_bank[:], 1.0 / SHARE_SCALE, f[:], ALU.mult, ALU.mult,
+                                       accum_out=z_scaled[:])
+        px_groups = px[:].rearrange("p (g j) -> p g j", j=GROUP)
         s1g = sb.tile([P, G], F32)
-        gh = G // HALVES
-        nc.vector.tensor_reduce(s1g[:, :gh], px3[:, :gh, :], AX.X, ALU.add)
-        rz = sb.tile([P, 1], F32)
-        nc.vector.reciprocal(rz[:], z256[:])
-        for h in range(1, HALVES):
-            nc.vector.tensor_reduce(s1g[:, h * gh : (h + 1) * gh], px3[:, h * gh : (h + 1) * gh, :], AX.X, ALU.add)
-        c = sb.tile([P, 1], F32)
-        nc.scalar.mul(c[:], rz[:], 2.0)
-        nf = sb.tile([P, NB], F32)
+        nc.vector.tensor_reduce(s1g[:, :HALF_GROUPS], px_groups[:, :HALF_GROUPS, :], AX.X, ALU.add)
+        to_share = sb.tile([P, 1], F32)
+        nc.vector.reciprocal(to_share[:], z_scaled[:])
+        to_ds1g = sb.tile([P, 1], F32)
+        nc.scalar.mul(to_ds1g[:], to_share[:], 2.0)
+        to_dz = sb.tile([P, BANKS], F32)
         neg_rz = sb.tile([P, 1], F32)
-        nc.scalar.mul(neg_rz[:], rz[:], -1.0 / 256.0)
-        nc.scalar.activation(nf[:], f[:], ACT.Identity, scale=neg_rz[:])
-
+        nc.scalar.mul(neg_rz[:], to_share[:], -1.0 / SHARE_SCALE)
+        nc.scalar.activation(to_dz[:], f[:], ACT.Identity, scale=neg_rz[:])
         u1 = sb.tile([P, G], F32)
-        nc.vector.scalar_tensor_tensor(u1[:], s1g[:], rz[:], aim_sb[:], ALU.mult, ALU.subtract)
         e2 = sb.tile([P, I], F32)
-        e_sum = sb.tile([P, 1], F32)
-        nc.vector.scalar_tensor_tensor(e2[:].rearrange("p (g j) -> p g j", j=8),
-                                       u1[:].unsqueeze(2).to_broadcast([P, G, 8]), c[:], px3,
-                                       ALU.mult, ALU.mult, accum_out=e_sum[:])
+        e2_groups = e2[:].rearrange("p (g j) -> p g j", j=GROUP)
+        e2_sums = sb.tile([P, 2], F32)
+
+        def form_u1(h):
+            groups = slice(h * HALF_GROUPS, (h + 1) * HALF_GROUPS)
+            nc.vector.scalar_tensor_tensor(u1[:, groups], s1g[:, groups], to_share[:], aim_sb[:, groups],
+                                           ALU.mult, ALU.subtract)
+
+        def form_e2(h):
+            groups = slice(h * HALF_GROUPS, (h + 1) * HALF_GROUPS)
+            nc.vector.scalar_tensor_tensor(e2_groups[:, groups, :],
+                                           u1[:, groups].unsqueeze(2).to_broadcast([P, HALF_GROUPS, GROUP]),
+                                           to_ds1g[:], px_groups[:, groups, :], ALU.mult, ALU.mult,
+                                           accum_out=e2_sums[:, h : h + 1])
+
+        form_u1(0)
+        nc.vector.tensor_reduce(s1g[:, HALF_GROUPS:], px_groups[:, HALF_GROUPS:, :], AX.X, ALU.add)
+        form_e2(0)
+        form_u1(1)
+        form_e2(1)
         nc.vector.tensor_copy(s2[:].indirect(offsets[:]), e2[:])
 
-        dzb = sb.tile([P, NB], F32)
-        nc.scalar.activation(dzb[:], nf[:], ACT.Identity, scale=e_sum[:])
+        dz_bank = sb.tile([P, BANKS], F32)
+        dz_first = sb.tile([P, BANKS], F32)
+        nc.scalar.activation(dz_first[:], to_dz[:], ACT.Identity, scale=e2_sums[:, 0:1])
+        for pair in zip(TENSOR_BANKS, GPSIMD_BANKS):
+            for b in pair:
+                nc.scalar.activation(dz_bank[:, b : b + 1], e2_sums[:, 1:2], ACT.Identity,
+                                     scale=to_dz[:, b : b + 1], bias=dz_first[:, b : b + 1])
+
+        def scale_on_scalar(dz_p, b, lo, hi):
+            nc.scalar.activation(dz_p[:, lo:hi], p[:, bank_cols(b, lo, hi)], ACT.Identity, scale=dz_bank[:, b : b + 1])
+
+        def scale_on_gpsimd(dz_p, b, lo, hi):
+            nc.gpsimd.tensor_scalar(dz_p[:, lo:hi], p[:, bank_cols(b, lo, hi)], dz_bank[:, b : b + 1], 0.0,
+                                    ALU.mult, ALU.add)
+
         base = {}
-
-        def turn_in(b):
-            pd = sb.tile([P, BANK], F32, name=f"pd{b}")
-            nc.scalar.activation(pd[:], p[:, b * BANK : (b + 1) * BANK], ACT.Identity, scale=dzb[:, b : b + 1])
-            for j in range(4):
-                nc.tensor.matmul(turned[b][:, j * P : (j + 1) * P], pd[:, j * P : (j + 1) * P], ident[:],
-                                 start=False, stop=(j == 3), is_transpose=True)
-
-        def turn_back(b):
-            tsb = sb.tile([P, BANK], F32, name=f"tsb{b}")
-            nc.scalar.copy(tsb[:], turned[b][:])
-            base[b] = ps.tile([P, BANK], F32, name=f"score{b}")
-            for j in range(4):
-                nc.tensor.transpose(base[b][:, j * P : (j + 1) * P], tsb[:, j * P : (j + 1) * P], ident[:])
-
-        for b in PE_CHUNKS[:2]:
-            turn_in(b)
-        for b in SHADOW:
-            pd = sb.tile([P, BANK], F32, name=f"pd{b}")
-            nc.scalar.activation(pd[:], p[:, b * BANK : (b + 1) * BANK], ACT.Identity, scale=dzb[:, b : b + 1])
+        for b in TENSOR_BANKS:
+            dz_p = sb.tile([P, BANK], F32, name=f"dz_p{b}")
+            for h in range(2):
+                scale_on_scalar(dz_p, b, h * PIECE, (h + 1) * PIECE)
+                for j in range(2):
+                    nc.tensor.matmul(turned[b, h][:, j * P : (j + 1) * P],
+                                     dz_p[:, h * PIECE + j * P : h * PIECE + (j + 1) * P], ident[:],
+                                     start=False, stop=(j == 1), is_transpose=True)
+        for b in GPSIMD_BANKS:
+            dz_p = sb.tile([P, BANK], F32, name=f"dz_p{b}")
+            from_col = PIECE if b == LAST else 0
+            if from_col:
+                scale_on_scalar(dz_p, b, 0, from_col)
+            scale_on_gpsimd(dz_p, b, from_col, BANK)
             base[b] = sb.tile([P, BANK], F32, name=f"base{b}")
-            nc.gpsimd.tensor_tensor(base[b][:], pd[:], old_cols(b, 0, BANK), ALU.add)
-        turn_back(PE_CHUNKS[0])
-        for b in PE_CHUNKS[2:]:
-            turn_in(b)
-        for b in PE_CHUNKS[1:]:
-            turn_back(b)
-        for b in G_CHUNKS:
-            base[b] = sb.tile([P, BANK], F32, name=f"pd{SHADOW[-1]}")
-            nc.gpsimd.tensor_tensor(base[b][:], s2[:, b * BANK : (b + 1) * BANK], old_cols(b, 0, BANK), ALU.add)
-        y_tail = sb.tile([P, 2 * BANK], F32, name=f"tsb{PE_CHUNKS[-1]}")
-        for b, lo, hi in OUT_ORDER:
-            cols = slice(b * BANK + lo, b * BANK + hi)
-            if b in PE_CHUNKS:
-                y = sb.tile([P, hi - lo], F32, name=f"y{b}_{lo}")
+            nc.gpsimd.tensor_tensor(base[b][:], dz_p[:], old_cols(b), ALU.add)
+        for b in TENSOR_BANKS:
+            staged = sb.tile([P, BANK], F32, name=f"staged{b}")
+            base[b] = ps.tile([P, BANK], F32, name=f"bank{b}")
+            for h in range(2):
+                nc.scalar.copy(staged[:, h * PIECE : (h + 1) * PIECE], turned[b, h][:])
+                for j in range(2):
+                    block = slice(h * PIECE + j * P, h * PIECE + (j + 1) * P)
+                    nc.tensor.transpose(base[b][:, block], staged[:, block], ident[:])
+
+        y_late = sb.tile([P, len(GPSIMD_BANKS) * BANK], F32, name=f"staged{TENSOR_BANKS[-1]}")
+        for b in range(BANKS):
+            cols = bank_cols(b)
+            if b in TENSOR_BANKS:
+                y = sb.tile([P, BANK], F32, name=f"y{b}")[:]
             else:
-                y = y_tail[:, (b - 2) * BANK + lo : (b - 2) * BANK + hi]
-            if b in G_CHUNKS:
-                nc.vector.scalar_tensor_tensor(y[:], p[:, cols], dzb[:, b : b + 1], base[b][:, lo:hi], ALU.mult, ALU.add)
-            else:
-                nc.vector.tensor_tensor(y[:], base[b][:, lo:hi], s2[:, cols], ALU.add)
-            nc.sync.dma_start(out[:, cols], y[:])
+                y = y_late[:, bank_cols(b - GPSIMD_BANKS[0])]
+            nc.vector.tensor_tensor(y, base[b][:], s2[:, cols], ALU.add)
+            queue = nc.sync if b % 2 == 0 else nc.scalar
+            queue.dma_start(out[:, cols], y)

from contextlib import ExitStack

import concourse.mybir as mybir
from concourse.masks import make_identity

D, V, Q, I, G = 512, 2048, 128, 512, 64
FLOPS = 2 * D * V * Q

F32 = mybir.dt.float32
BF16 = mybir.dt.bfloat16
I32 = mybir.dt.int32
U32 = mybir.dt.uint32
U16 = mybir.dt.uint16
U8 = mybir.dt.uint8
FP8X4 = mybir.dt.float8_e4m3fn_x4
FP4X4 = mybir.dt.float4_e2m1fn_x4
ALU = mybir.AluOpType
ACT = mybir.ActivationFunctionType
AX = mybir.AxisListType

P = 128
PACK = 4
FP4_WORD_BYTES = 2
LIST_ROWS = 16
GROUP = I // G
SHARE_SCALE = 256.0
BANK = 512
BANKS = V // BANK
LAST = BANKS - 1
PIECE = BANK // 2
WORD_LOADS = ((0, 512), (512, 1024), (1024, 2048))
TENSOR_BANKS = (0, 1)
GPSIMD_BANKS = (2, 3)
HALF_SLOTS = I // 2
HALF_GROUPS = G // 2


def bank_cols(b, lo=0, hi=BANK):
    return slice(b * BANK + lo, b * BANK + hi)


def tile_attend_bgroupaims_heads_kernel(tc, hid, voc_words, voc_scales, aim, old, offs, out):
    nc = tc.nc
    with ExitStack() as ctx:
        lists = ctx.enter_context(tc.tile_pool(name="lists", bufs=1))
        sb = ctx.enter_context(tc.tile_pool(name="sb", bufs=1))
        ps = ctx.enter_context(tc.psum_pool(name="ps", bufs=1))

        hid_raw = sb.tile([P, PACK, Q], F32)
        nc.sync.dma_start(hid_raw[:], hid.rearrange("(p t) q -> p t q", t=PACK))
        voc_plane = sb.tile([P, V], U8, align_bytes=64)
        for r in range(4):
            nc.sync.dma_start(voc_plane[r:P:32, :].bitcast(I32), voc_scales[0, r:16:4, :].bitcast(I32))
        words = {}
        for lo, hi in WORD_LOADS:
            loaded = sb.tile([P, FP4_WORD_BYTES * (hi - lo)], U8, align_bytes=64, name=f"words{lo}")
            nc.sync.dma_start(loaded[:].bitcast(I32),
                              voc_words[0, :, FP4_WORD_BYTES * lo : FP4_WORD_BYTES * hi].bitcast(I32))
            for b in range(lo // BANK, hi // BANK):
                words[b] = loaded[:, FP4_WORD_BYTES * (b * BANK - lo) : FP4_WORD_BYTES * ((b + 1) * BANK - lo)]
        offsets = lists.tile([P, I // LIST_ROWS], U16)
        nc.sync.dma_start(offsets[:], offs)
        old_pairs = [sb.tile([P, 2 * BANK], F32, name=f"old{pair}") for pair in range(BANKS // 2)]
        for pair in range(BANKS // 2):
            nc.sync.dma_start(old_pairs[pair][:], old[:, 2 * pair * BANK : 2 * (pair + 1) * BANK])
        aim_sb = sb.tile([P, G], F32)
        nc.sync.dma_start(aim_sb[:], aim)

        def old_cols(b, lo=0, hi=BANK):
            return old_pairs[b // 2][:, bank_cols(b % 2, lo, hi)]

        s2 = sb.tile([P, V], F32)
        nc.vector.memset(s2[:], 0.0)
        ident = sb.tile([P, P], F32)
        make_identity(nc, ident[:])

        hid_bf = sb.tile([P, Q, PACK], BF16, align_bytes=64)
        nc.vector.tensor_copy(hid_bf[:].rearrange("p (c i) t -> p c t i", i=4),
                              hid_raw[:].rearrange("p t (c i) -> p c t i", i=4))
        hid_codes = sb.tile([P, Q], U32, align_bytes=64)
        hid_plane = sb.tile([P, Q], U8, align_bytes=64)
        nc.vector.quantize_mx(out=hid_codes[:].bitcast(FP8X4), scales=hid_plane[:],
                              in_=hid_bf[:].rearrange("p q t -> p (q t)"))

        a = sb.tile([P, V], F32)
        p = sb.tile([P, V], F32)
        m = sb.tile([P, BANKS], F32)
        neg_m = sb.tile([P, BANKS], F32)
        z_bank = sb.tile([P, BANKS], F32)
        neg_m1 = sb.tile([P, 1], F32)
        f = sb.tile([P, BANKS], F32)
        nc.vector.memset(f[:, LAST:], 1.0)
        for b in range(BANKS):
            cols = bank_cols(b)
            scores = ps.tile([P, BANK], F32, name=f"bank{b}")
            nc.tensor.matmul_mx(out=scores[:], lhsT=hid_codes[:].bitcast(FP8X4), lhsT_scale=hid_plane[:],
                                rhs=words[b].bitcast(FP4X4), rhs_scale=voc_plane[:, cols], start=True, stop=True)
            nc.vector.tensor_scalar(a[:, cols], scores[:], 1.0, None, ALU.mult, ALU.max, accum_out=m[:, b : b + 1])
            if b < LAST:
                nc.gpsimd.tensor_scalar(neg_m[:, b : b + 1], m[:, b : b + 1], -1.0, 0.0, ALU.mult, ALU.add)
                shift = neg_m[:, b : b + 1]
            else:
                nc.vector.tensor_reduce(neg_m1[:], m[:], AX.X, ALU.max, negate=True)
                shift = neg_m1[:]
                nc.scalar.activation(f[:, :LAST], m[:, :LAST], ACT.Exp, bias=neg_m1[:])
            nc.scalar.activation(p[:, cols], a[:, cols], ACT.Exp, bias=shift, accum_out=z_bank[:, b : b + 1])

        turned = {}
        for b in TENSOR_BANKS:
            for h in range(2):
                turned[b, h] = ps.tile([P, PIECE], F32, name=f"turned{b}_{h}")
                for j in range(2):
                    nc.tensor.matmul(turned[b, h][:, j * P : (j + 1) * P],
                                     old_cols(b, h * PIECE + j * P, h * PIECE + (j + 1) * P), ident[:],
                                     start=(j == 0), stop=False, is_transpose=True)

        a_listed = sb.tile([P, I], F32)
        px = sb.tile([P, I], F32)
        for h in range(2):
            slots = slice(h * HALF_SLOTS, (h + 1) * HALF_SLOTS)
            half_list = offsets[:, h * HALF_SLOTS // LIST_ROWS : (h + 1) * HALF_SLOTS // LIST_ROWS]
            nc.vector.tensor_copy(a_listed[:, slots].bitcast(U32), a[:].bitcast(U32).indirect(half_list))
            nc.scalar.activation(px[:, slots], a_listed[:, slots], ACT.Exp, bias=neg_m1[:])

        z_terms = sb.tile([P, BANKS], F32)
        z_scaled = sb.tile([P, 1], F32)
        nc.vector.scalar_tensor_tensor(z_terms[:], z_bank[:], 1.0 / SHARE_SCALE, f[:], ALU.mult, ALU.mult,
                                       accum_out=z_scaled[:])
        px_groups = px[:].rearrange("p (g j) -> p g j", j=GROUP)
        s1g = sb.tile([P, G], F32)
        nc.vector.tensor_reduce(s1g[:, :HALF_GROUPS], px_groups[:, :HALF_GROUPS, :], AX.X, ALU.add)
        to_share = sb.tile([P, 1], F32)
        nc.vector.reciprocal(to_share[:], z_scaled[:])
        to_ds1g = sb.tile([P, 1], F32)
        nc.scalar.mul(to_ds1g[:], to_share[:], 2.0)
        to_dz = sb.tile([P, BANKS], F32)
        neg_rz = sb.tile([P, 1], F32)
        nc.scalar.mul(neg_rz[:], to_share[:], -1.0 / SHARE_SCALE)
        nc.scalar.activation(to_dz[:], f[:], ACT.Identity, scale=neg_rz[:])
        u1 = sb.tile([P, G], F32)
        e2 = sb.tile([P, I], F32)
        e2_groups = e2[:].rearrange("p (g j) -> p g j", j=GROUP)
        e2_sums = sb.tile([P, 2], F32)

        def form_u1(h):
            groups = slice(h * HALF_GROUPS, (h + 1) * HALF_GROUPS)
            nc.vector.scalar_tensor_tensor(u1[:, groups], s1g[:, groups], to_share[:], aim_sb[:, groups],
                                           ALU.mult, ALU.subtract)

        def form_e2(h):
            groups = slice(h * HALF_GROUPS, (h + 1) * HALF_GROUPS)
            nc.vector.scalar_tensor_tensor(e2_groups[:, groups, :],
                                           u1[:, groups].unsqueeze(2).to_broadcast([P, HALF_GROUPS, GROUP]),
                                           to_ds1g[:], px_groups[:, groups, :], ALU.mult, ALU.mult,
                                           accum_out=e2_sums[:, h : h + 1])

        form_u1(0)
        nc.vector.tensor_reduce(s1g[:, HALF_GROUPS:], px_groups[:, HALF_GROUPS:, :], AX.X, ALU.add)
        form_e2(0)
        form_u1(1)
        form_e2(1)
        nc.vector.tensor_copy(s2[:].indirect(offsets[:]), e2[:])

        dz_bank = sb.tile([P, BANKS], F32)
        dz_first = sb.tile([P, BANKS], F32)
        nc.scalar.activation(dz_first[:], to_dz[:], ACT.Identity, scale=e2_sums[:, 0:1])
        for pair in zip(TENSOR_BANKS, GPSIMD_BANKS):
            for b in pair:
                nc.scalar.activation(dz_bank[:, b : b + 1], e2_sums[:, 1:2], ACT.Identity,
                                     scale=to_dz[:, b : b + 1], bias=dz_first[:, b : b + 1])

        def scale_on_scalar(dz_p, b, lo, hi):
            nc.scalar.activation(dz_p[:, lo:hi], p[:, bank_cols(b, lo, hi)], ACT.Identity, scale=dz_bank[:, b : b + 1])

        def scale_on_gpsimd(dz_p, b, lo, hi):
            nc.gpsimd.tensor_scalar(dz_p[:, lo:hi], p[:, bank_cols(b, lo, hi)], dz_bank[:, b : b + 1], 0.0,
                                    ALU.mult, ALU.add)

        base = {}
        for b in TENSOR_BANKS:
            dz_p = sb.tile([P, BANK], F32, name=f"dz_p{b}")
            for h in range(2):
                scale_on_scalar(dz_p, b, h * PIECE, (h + 1) * PIECE)
                for j in range(2):
                    nc.tensor.matmul(turned[b, h][:, j * P : (j + 1) * P],
                                     dz_p[:, h * PIECE + j * P : h * PIECE + (j + 1) * P], ident[:],
                                     start=False, stop=(j == 1), is_transpose=True)
        for b in GPSIMD_BANKS:
            dz_p = sb.tile([P, BANK], F32, name=f"dz_p{b}")
            from_col = PIECE if b == LAST else 0
            if from_col:
                scale_on_scalar(dz_p, b, 0, from_col)
            scale_on_gpsimd(dz_p, b, from_col, BANK)
            base[b] = sb.tile([P, BANK], F32, name=f"base{b}")
            nc.gpsimd.tensor_tensor(base[b][:], dz_p[:], old_cols(b), ALU.add)
        for b in TENSOR_BANKS:
            staged = sb.tile([P, BANK], F32, name=f"staged{b}")
            base[b] = ps.tile([P, BANK], F32, name=f"bank{b}")
            for h in range(2):
                nc.scalar.copy(staged[:, h * PIECE : (h + 1) * PIECE], turned[b, h][:])
                for j in range(2):
                    block = slice(h * PIECE + j * P, h * PIECE + (j + 1) * P)
                    nc.tensor.transpose(base[b][:, block], staged[:, block], ident[:])

        y_late = sb.tile([P, len(GPSIMD_BANKS) * BANK], F32, name=f"staged{TENSOR_BANKS[-1]}")
        for b in range(BANKS):
            cols = bank_cols(b)
            if b in TENSOR_BANKS:
                y = sb.tile([P, BANK], F32, name=f"y{b}")[:]
            else:
                y = y_late[:, bank_cols(b - GPSIMD_BANKS[0])]
            nc.vector.tensor_tensor(y, base[b][:], s2[:, cols], ALU.add)
            queue = nc.sync if b % 2 == 0 else nc.scalar
            queue.dma_start(out[:, cols], y)
